import numpy as np
import ml_dtypes


def mxq(x, axis, fmt="e4m3"):
    dtype, down = {"e4m3": (ml_dtypes.float8_e4m3fn, 7), "e5m2": (ml_dtypes.float8_e5m2, 14)}[fmt]
    v = np.moveaxis(np.asarray(x, np.float32).astype(ml_dtypes.bfloat16).astype(np.float64), axis, -1)
    blocks = v.reshape(v.shape[:-1] + (-1, 32))
    amax = np.abs(blocks).max(-1, keepdims=True)
    byte = np.maximum(np.where(amax > 0, np.frexp(amax)[1] - 1 + 127, 0) - down, 1)
    scale = np.exp2(byte - 127.0)
    codes = (blocks / scale).astype(np.float32).astype(dtype).astype(np.float64)
    return np.moveaxis((codes * scale).reshape(v.shape), -1, axis)


WIDE = False


def mx_kscale(k):
    if not WIDE:
        return np.ones(k)
    levels = np.array([10, -10, 5, -5, 0])
    if k % 512:
        return np.exp2(np.random.permutation(np.resize(levels, k // 32))).repeat(32)
    a = np.empty((k // 512, 16))
    for p in range(k // 512):
        a[p, :8] = np.random.permutation(np.resize(levels, 8))
        for g in range(8):
            far = levels[np.abs(levels - a[p, g]) >= 10]
            a[p, g + 8] = far[np.random.randint(len(far))]
    return np.exp2(a.ravel()).repeat(32)


def f64(x):
    return np.asarray(x).astype(np.float64)


def striped(idx):
    return np.tile(idx.reshape(-1, 16).T, (8, 1)).astype(np.uint16)


def unstriped(offs):
    return offs[:16].T.reshape(-1).astype(np.int64)


K, T, E, C, N = 1024, 1024, 16, 128, 128


def by_expert(wq, xq):
    return np.concatenate([wq[e].T @ xq[:, e * C:(e + 1) * C] for e in range(E)], axis=1)


def setup_inputs():
    n = np.random.standard_normal
    s = mx_kscale(K)[:, None]
    first = np.random.permutation(np.repeat(np.arange(E), T // E))
    second = (first + 1 + np.random.permutation(np.repeat(np.arange(E - 1), -(-T // (E - 1)))[:T])) % E
    while np.bincount(second, minlength=E).max() != T // E:
        load = np.bincount(second, minlength=E); hi, lo = int(load.argmax()), int(load.argmin())
        t = np.flatnonzero((second == hi) & (first != lo))[0]; second[t] = lo
    slot_token = np.empty(E * C, np.int64); pos = np.empty((2, T), np.int64); fill = np.zeros(E, np.int64)
    place = np.stack([np.random.permutation(C) for _ in range(E)])
    for r, deal in enumerate((first, second)):
        for t in np.random.permutation(T):
            e = deal[t]; j = e * C + place[e, fill[e]]; fill[e] += 1; slot_token[j] = t; pos[r, t] = j
    g = np.random.uniform(0.2, 0.8, T)
    return {
        "xT": (n((K, T)) * s).astype(np.float32),
        "w": (n((E, K, N)) / np.sqrt(K) / s[None]).astype(np.float32),
        "gate": np.stack([np.tile(g, (N, 1)), np.tile(1.0 - g, (N, 1))]).astype(np.float32),
        "offs": striped(slot_token),
        "pos1": striped(pos[0]),
        "pos2": striped(pos[1]),
    }


def reference(xT, w, gate, offs, pos1, pos2):
    idx = unstriped(offs)
    xq = mxq(f64(xT)[:, idx], 0, "e4m3")
    y = by_expert(mxq(f64(w), 1, "e4m3"), xq)
    return f64(gate[0]) * y[:, unstriped(pos1)] + f64(gate[1]) * y[:, unstriped(pos2)]

@@ -1,0 +1,181 @@
+from contextlib import ExitStack
+
+import concourse.mybir as mybir
+
+K, T, E, C, N = 1024, 1024, 16, 128, 128
+FLOPS = 2 * K * N * E * C
+
+F32 = mybir.dt.float32
+BF16 = mybir.dt.bfloat16
+U32 = mybir.dt.uint32
+U16 = mybir.dt.uint16
+U8 = mybir.dt.uint8
+FP8X4 = mybir.dt.float8_e4m3fn_x4
+MULT = mybir.AluOpType.mult
+ADD = mybir.AluOpType.add
+
+P = 128
+PACK = 4
+PASSES = K // (P * PACK)
+HALF = 512
+CHUNKS = (768, 768, 512)
+X_VEC = ((352, 352), (0, 0))
+G_EXPERTS = (0, 2, 4, 6, 8)
+V_EXPERTS = ()
+SPLIT = {14: ("vs", False), 15: ("sv", True)}
+GROUPS = ((0, 1, 2, 3), (4, 5, 6, 7), (8, 9, 10, 11), (12, 13), (14,), (15,))
+BANKS = 4
+V_BANKS = (3,)
+PIECES = (384, 384, 256)
+
+
+def tile_routed_moe_kernel(tc, xT, w, gate, offs, pos1, pos2, out):
+    nc = tc.nc
+    with ExitStack() as ctx:
+        lists = ctx.enter_context(tc.tile_pool(name="lists", bufs=1))
+        keep = ctx.enter_context(tc.tile_pool(name="keep", bufs=1))
+        psum = ctx.enter_context(tc.psum_pool(name="psum", bufs=1))
+
+        offs_t = lists.tile([P, E * C // 16], U16, name="offs_t")
+        nc.sync.dma_start(offs_t[:], offs)
+        xv = xT.rearrange("(a p j) t -> a p j t", p=P, j=PACK)
+        xr = {}
+        for a in range(PASSES):
+            for h in range(T // HALF):
+                xr[a, h] = keep.tile([P, PACK, HALF], F32, name="xr%d%d" % (a, h))
+                nc.sync.dma_start(out=xr[a, h][:], in_=xv[a, :, :, h * HALF:(h + 1) * HALF])
+        wv = w.rearrange("e (a p j) n -> e p a (j n)", p=P, j=PACK)
+        wr = {}
+        for e in range(E):
+            wr[e] = keep.tile([P, PASSES, PACK * N], F32, name="wr%d" % e)
+            if e in SPLIT:
+                for a in range(PASSES):
+                    nc.sync.dma_start(out=wr[e][:, a, :], in_=wv[e, :, a, :])
+            else:
+                nc.sync.dma_start(out=wr[e][:], in_=wv[e])
+        pos1_t = lists.tile([P, T // 16], U16, name="pos1_t")
+        nc.sync.dma_start(pos1_t[:], pos1)
+        pos2_t = lists.tile([P, T // 16], U16, name="pos2_t")
+        nc.sync.dma_start(pos2_t[:], pos2)
+        g_t = []
+        for r in range(2):
+            g_r = keep.tile([P, T], F32, name="g%d" % r)
+            nc.sync.dma_start(out=g_r[:], in_=gate[r])
+            g_t.append(g_r)
+
+        warm = keep.tile([P, 8], F32, name="warm")
+        nc.vector.memset(warm[:], 0.0)
+        warm2 = keep.tile([P, 8], F32, name="warm2")
+        nc.scalar.copy(out=warm2[:], in_=warm[:])
+        xw = [keep.tile([P, T], U32, name="xw%d" % a, align_bytes=64) for a in range(PASSES)]
+        xs = keep.tile([P, T], U8, name="xs", align_bytes=64)
+        nc.gpsimd.memset(xs[:], 0)
+
+        gw, gs, o_c, where = [], [], [], {}
+        s0 = 0
+        for c, n_s in enumerate(CHUNKS):
+            gw.append([keep.tile([P, n_s], U32, name="gw%d_%d" % (a, c), align_bytes=64) for a in range(PASSES)])
+            gs.append(keep.tile([P, n_s], U8, name="gs%d" % c, align_bytes=64))
+            o_c.append(offs_t[:, s0 // 16:(s0 + n_s) // 16])
+            for e in range(s0 // C, (s0 + n_s) // C):
+                where[e] = (c, e * C - s0)
+            s0 += n_s
+
+        def tokens(a):
+            for h in range(T // HALF):
+                xg = keep.tile([P, HALF, PACK], BF16, name="xg%d%d" % (a, h), align_bytes=64)
+                n_v = X_VEC[a][h]
+                if n_v > 0:
+                    nc.vector.tensor_copy(
+                        out=xg[:, 0:n_v, :].rearrange("p (c i) j -> p c j i", i=4),
+                        in_=xr[a, h][:, :, 0:n_v].rearrange("p j (c i) -> p c j i", i=4),
+                    )
+                nc.scalar.copy(
+                    out=xg[:, n_v:HALF, :].rearrange("p (c i) j -> p c j i", i=4),
+                    in_=xr[a, h][:, :, n_v:HALF].rearrange("p j (c i) -> p c j i", i=4),
+                )
+                cols = slice(h * HALF, (h + 1) * HALF)
+                nc.vector.quantize_mx(
+                    out=xw[a][:, cols].bitcast(FP8X4),
+                    scales=xs[4 * a:P, cols],
+                    in_=xg[:].rearrange("p t j -> p (t j)"),
+                )
+
+        tokens(0)
+        for c in range(len(CHUNKS)):
+            nc.vector.tensor_copy(out=gw[c][0][:], in_=xw[0][:].indirect(o_c[c]))
+        tokens(1)
+        for c in range(len(CHUNKS)):
+            nc.vector.tensor_copy(out=gw[c][1][:], in_=xw[1][:].indirect(o_c[c]))
+            nc.vector.tensor_copy(out=gs[c][:], in_=xs[:].indirect(o_c[c]))
+
+        acc = [psum.tile([P, E // BANKS, C], F32, name="acc%d" % b) for b in range(BANKS)]
+        for gi, grp in enumerate(GROUPS):
+            n_e = len(grp)
+            wg = keep.tile([P, n_e, PASSES, N * PACK], BF16, name="wg%d" % gi, align_bytes=64)
+            wc = keep.tile([P, n_e, PASSES, N], U32, name="wc%d" % gi, align_bytes=64)
+            ws = keep.tile([P, n_e, PASSES, N], U8, name="ws%d" % gi, align_bytes=64)
+            for i, e in enumerate(grp):
+                if e in SPLIT:
+                    for a in range(PASSES):
+                        dst = wg[:, i, a, :].rearrange("p (c i j) -> p c j i", i=4, j=PACK)
+                        src = wr[e][:, a, :].rearrange("p (j c i) -> p c j i", i=4, j=PACK)
+                        if SPLIT[e][0][a] == "v":
+                            nc.vector.tensor_copy(out=dst, in_=src)
+                        else:
+                            nc.scalar.copy(out=dst, in_=src)
+                        if SPLIT[e][1]:
+                            nc.vector.quantize_mx(
+                                out=wc[:, i, a, :].bitcast(FP8X4), scales=ws[:, i, a, :], in_=wg[:, i, a, :]
+                            )
+                elif e in G_EXPERTS:
+                    nc.gpsimd.tensor_scalar(
+                        out=wg[:, i, :, :].rearrange("p a (n j) -> p a n j", j=PACK),
+                        in0=wr[e][:].rearrange("p a (j n) -> p a n j", j=PACK),
+                        scalar1=1.0, scalar2=0.0, op0=MULT, op1=ADD,
+                    )
+                else:
+                    dst = wg[:, i, :, :].rearrange("p a (c i j) -> p a c j i", i=4, j=PACK)
+                    src = wr[e][:].rearrange("p a (j c i) -> p a c j i", i=4, j=PACK)
+                    if e in V_EXPERTS:
+                        nc.vector.tensor_copy(out=dst, in_=src)
+                    else:
+                        nc.scalar.copy(out=dst, in_=src)
+            if grp[0] not in SPLIT or not SPLIT[grp[0]][1]:
+                nc.vector.quantize_mx(
+                    out=wc[:].rearrange("p e a n -> p (e a n)").bitcast(FP8X4),
+                    scales=ws[:].rearrange("p e a n -> p (e a n)"),
+                    in_=wg[:].rearrange("p e a m -> p (e a m)"),
+                )
+            for i, e in enumerate(grp):
+                c, s = where[e]
+                for a in range(PASSES):
+                    nc.tensor.matmul_mx(
+                        out=acc[e % BANKS][:, e // BANKS, :],
+                        lhsT=wc[:, i, a, :].bitcast(FP8X4),
+                        lhsT_scale=ws[:, i, a, :],
+                        rhs=gw[c][a][:, s:s + C].bitcast(FP8X4),
+                        rhs_scale=gs[c][4 * a:P, s:s + C],
+                        start=(a == 0),
+                        stop=(a == PASSES - 1),
+                    )
+
+        y = keep.tile([P, E * C], F32, name="y")
+        y_by_bank = y[:].rearrange("p (i b c) -> p b i c", b=BANKS, c=C)
+        for b in range(BANKS):
+            if b in V_BANKS:
+                nc.vector.tensor_copy(out=y_by_bank[:, b], in_=acc[b][:])
+            else:
+                nc.scalar.copy(out=y_by_bank[:, b], in_=acc[b][:])
+
+        t1 = keep.tile([P, T], F32, name="t1")
+        t2 = keep.tile([P, T], F32, name="t2")
+        res = keep.tile([P, T], F32, name="res")
+        nc.vector.tensor_tensor(out=t1[:], in0=y[:].indirect(pos1_t[:]), in1=g_t[0][:], op=MULT)
+        nc.vector.tensor_tensor(out=t2[:], in0=y[:].indirect(pos2_t[:]), in1=g_t[1][:], op=MULT)
+        t0 = 0
+        for n_t in PIECES:
+            cols = slice(t0, t0 + n_t)
+            nc.vector.tensor_tensor(out=res[:, cols], in0=t1[:, cols], in1=t2[:, cols], op=ADD)
+            nc.sync.dma_start(out=out[:, cols], in_=res[:, cols])
+            t0 += n_t

@@ -20,7 +20,7 @@ PASSES = K // (P * PACK)
 HALF = 512
 CHUNKS = (768, 768, 512)
 X_VEC = ((352, 352), (0, 0))
-G_EXPERTS = (0, 2, 4, 6, 8)
+G_EXPERTS = (3, 5, 7)
 V_EXPERTS = ()
 SPLIT = {14: ("vs", False), 15: ("sv", True)}
 GROUPS = ((0, 1, 2, 3), (4, 5, 6, 7), (8, 9, 10, 11), (12, 13), (14,), (15,))

@@ -172,10 +172,11 @@ def tile_routed_moe_kernel(tc, xT, w, gate, offs, pos1, pos2, out):
         t2 = keep.tile([P, T], F32, name="t2")
         res = keep.tile([P, T], F32, name="res")
         nc.vector.tensor_tensor(out=t1[:], in0=y[:].indirect(pos1_t[:]), in1=g_t[0][:], op=MULT)
-        nc.vector.tensor_tensor(out=t2[:], in0=y[:].indirect(pos2_t[:]), in1=g_t[1][:], op=MULT)
         t0 = 0
         for n_t in PIECES:
             cols = slice(t0, t0 + n_t)
+            part = pos2_t[:, t0 // 16:(t0 + n_t) // 16]
+            nc.vector.tensor_tensor(out=t2[:, cols], in0=y[:].indirect(part), in1=g_t[1][:, cols], op=MULT)
             nc.vector.tensor_tensor(out=res[:, cols], in0=t1[:, cols], in1=t2[:, cols], op=ADD)
             nc.sync.dma_start(out=out[:, cols], in_=res[:, cols])
             t0 += n_t

@@ -19,7 +19,8 @@ PACK = 4
 PASSES = K // (P * PACK)
 HALF = 512
 CHUNKS = (768, 768, 512)
-X_VEC = ((352, 352), (0, 0))
+X_WHOLE = (0,)
+X_VEC = ((288, 288), (0, 0))
 G_EXPERTS = (3, 5, 7)
 V_EXPERTS = ()
 SPLIT = {14: ("vs", False), 15: ("sv", True)}
@@ -37,13 +38,21 @@ def tile_routed_moe_kernel(tc, xT, w, gate, offs, pos1, pos2, out):
         psum = ctx.enter_context(tc.psum_pool(name="psum", bufs=1))
 
         offs_t = lists.tile([P, E * C // 16], U16, name="offs_t")
-        nc.sync.dma_start(offs_t[:], offs)
         xv = xT.rearrange("(a p j) t -> a p j t", p=P, j=PACK)
         xr = {}
         for a in range(PASSES):
-            for h in range(T // HALF):
-                xr[a, h] = keep.tile([P, PACK, HALF], F32, name="xr%d%d" % (a, h))
-                nc.sync.dma_start(out=xr[a, h][:], in_=xv[a, :, :, h * HALF:(h + 1) * HALF])
+            if a in X_WHOLE:
+                whole = keep.tile([P, PACK, T], F32, name="xr%d" % a)
+                nc.sync.dma_start(out=whole[:], in_=xv[a])
+                for h in range(T // HALF):
+                    xr[a, h] = whole[:, :, h * HALF:(h + 1) * HALF]
+            else:
+                for h in range(T // HALF):
+                    part = keep.tile([P, PACK, HALF], F32, name="xr%d%d" % (a, h))
+                    nc.sync.dma_start(out=part[:], in_=xv[a, :, :, h * HALF:(h + 1) * HALF])
+                    xr[a, h] = part[:]
+            if a == 0:
+                nc.sync.dma_start(offs_t[:], offs)
         wv = w.rearrange("e (a p j) n -> e p a (j n)", p=P, j=PACK)
         wr = {}
         for e in range(E):

@@ -20,7 +20,7 @@ PASSES = K // (P * PACK)
 HALF = 512
 CHUNKS = (768, 768, 512)
 X_WHOLE = (0,)
-X_VEC = ((288, 288), (0, 0))
+X_VEC = ((320, 320), (0, 0))
 G_EXPERTS = (3, 5, 7)
 V_EXPERTS = ()
 SPLIT = {14: ("vs", False), 15: ("sv", True)}
@@ -181,11 +181,10 @@ def tile_routed_moe_kernel(tc, xT, w, gate, offs, pos1, pos2, out):
         t2 = keep.tile([P, T], F32, name="t2")
         res = keep.tile([P, T], F32, name="res")
         nc.vector.tensor_tensor(out=t1[:], in0=y[:].indirect(pos1_t[:]), in1=g_t[0][:], op=MULT)
+        nc.vector.tensor_tensor(out=t2[:], in0=y[:].indirect(pos2_t[:]), in1=g_t[1][:], op=MULT)
         t0 = 0
         for n_t in PIECES:
             cols = slice(t0, t0 + n_t)
-            part = pos2_t[:, t0 // 16:(t0 + n_t) // 16]
-            nc.vector.tensor_tensor(out=t2[:, cols], in0=y[:].indirect(part), in1=g_t[1][:, cols], op=MULT)
             nc.vector.tensor_tensor(out=res[:, cols], in0=t1[:, cols], in1=t2[:, cols], op=ADD)
             nc.sync.dma_start(out=out[:, cols], in_=res[:, cols])
             t0 += n_t

@@ -25,8 +25,9 @@ G_EXPERTS = (3, 5, 7)
 V_EXPERTS = ()
 SPLIT = {14: ("vs", False), 15: ("sv", True)}
 GROUPS = ((0, 1, 2, 3), (4, 5, 6, 7), (8, 9, 10, 11), (12, 13), (14,), (15,))
-BANKS = 4
-V_BANKS = (3,)
+BANKS = ((0, 4, 1), (4, 8, 1), (8, 16, 2), (9, 13, 2), (13, 16, 2))
+V_BANKS = (4,)
+Y_SHARES = (15, 0)
 PIECES = (384, 384, 256)
 
 
@@ -56,11 +57,13 @@ def tile_routed_moe_kernel(tc, xT, w, gate, offs, pos1, pos2, out):
         wv = w.rearrange("e (a p j) n -> e p a (j n)", p=P, j=PACK)
         wr = {}
         for e in range(E):
-            wr[e] = keep.tile([P, PASSES, PACK * N], F32, name="wr%d" % e)
             if e in SPLIT:
                 for a in range(PASSES):
-                    nc.sync.dma_start(out=wr[e][:, a, :], in_=wv[e, :, a, :])
+                    tag = "shared" if (e, a) == Y_SHARES else "wr%d_%d" % (e, a)
+                    wr[e, a] = keep.tile([P, PACK * N], F32, name="wr%d_%d" % (e, a), tag=tag, align_bytes=64)
+                    nc.sync.dma_start(out=wr[e, a][:], in_=wv[e, :, a, :])
             else:
+                wr[e] = keep.tile([P, PASSES, PACK * N], F32, name="wr%d" % e)
                 nc.sync.dma_start(out=wr[e][:], in_=wv[e])
         pos1_t = lists.tile([P, T // 16], U16, name="pos1_t")
         nc.sync.dma_start(pos1_t[:], pos1)
@@ -118,7 +121,12 @@ def tile_routed_moe_kernel(tc, xT, w, gate, offs, pos1, pos2, out):
             nc.vector.tensor_copy(out=gw[c][1][:], in_=xw[1][:].indirect(o_c[c]))
             nc.vector.tensor_copy(out=gs[c][:], in_=xs[:].indirect(o_c[c]))
 
-        acc = [psum.tile([P, E // BANKS, C], F32, name="acc%d" % b) for b in range(BANKS)]
+        acc, place = [], {}
+        for b, (first, end, step) in enumerate(BANKS):
+            experts = list(range(first, end, step))
+            acc.append(psum.tile([P, len(experts), C], F32, name="acc%d" % b))
+            for i, e in enumerate(experts):
+                place[e] = (b, i)
         for gi, grp in enumerate(GROUPS):
             n_e = len(grp)
             wg = keep.tile([P, n_e, PASSES, N * PACK], BF16, name="wg%d" % gi, align_bytes=64)
@@ -128,7 +136,7 @@ def tile_routed_moe_kernel(tc, xT, w, gate, offs, pos1, pos2, out):
                 if e in SPLIT:
                     for a in range(PASSES):
                         dst = wg[:, i, a, :].rearrange("p (c i j) -> p c j i", i=4, j=PACK)
-                        src = wr[e][:, a, :].rearrange("p (j c i) -> p c j i", i=4, j=PACK)
+                        src = wr[e, a][:].rearrange("p (j c i) -> p c j i", i=4, j=PACK)
                         if SPLIT[e][0][a] == "v":
                             nc.vector.tensor_copy(out=dst, in_=src)
                         else:
@@ -158,9 +166,10 @@ def tile_routed_moe_kernel(tc, xT, w, gate, offs, pos1, pos2, out):
                 )
             for i, e in enumerate(grp):
                 c, s = where[e]
+                b, slot = place[e]
                 for a in range(PASSES):
                     nc.tensor.matmul_mx(
-                        out=acc[e % BANKS][:, e // BANKS, :],
+                        out=acc[b][:, slot, :],
                         lhsT=wc[:, i, a, :].bitcast(FP8X4),
                         lhsT_scale=ws[:, i, a, :],
                         rhs=gw[c][a][:, s:s + C].bitcast(FP8X4),
@@ -169,13 +178,13 @@ def tile_routed_moe_kernel(tc, xT, w, gate, offs, pos1, pos2, out):
                         stop=(a == PASSES - 1),
                     )
 
-        y = keep.tile([P, E * C], F32, name="y")
-        y_by_bank = y[:].rearrange("p (i b c) -> p b i c", b=BANKS, c=C)
-        for b in range(BANKS):
+        y = keep.tile([P, E * C], F32, name="y", tag="shared", align_bytes=64)
+        y_by_expert = y[:].rearrange("p (e c) -> p e c", c=C)
+        for b, (first, end, step) in enumerate(BANKS):
             if b in V_BANKS:
-                nc.vector.tensor_copy(out=y_by_bank[:, b], in_=acc[b][:])
+                nc.vector.tensor_copy(out=y_by_expert[:, first:end:step], in_=acc[b][:])
             else:
-                nc.scalar.copy(out=y_by_bank[:, b], in_=acc[b][:])
+                nc.scalar.copy(out=y_by_expert[:, first:end:step], in_=acc[b][:])
 
         t1 = keep.tile([P, T], F32, name="t1")
         t2 = keep.tile([P, T], F32, name="t2")

from contextlib import ExitStack

import concourse.mybir as mybir

K, T, E, C, N = 1024, 1024, 16, 128, 128
FLOPS = 2 * K * N * E * C

F32 = mybir.dt.float32
BF16 = mybir.dt.bfloat16
U32 = mybir.dt.uint32
U16 = mybir.dt.uint16
U8 = mybir.dt.uint8
FP8X4 = mybir.dt.float8_e4m3fn_x4
MULT = mybir.AluOpType.mult
ADD = mybir.AluOpType.add

P = 128
PACK = 4
PASSES = K // (P * PACK)
HALF = 512
CHUNKS = (768, 768, 512)
X_WHOLE = (0,)
X_VEC = ((320, 320), (0, 0))
G_EXPERTS = (3, 5, 7)
V_EXPERTS = ()
SPLIT = {14: ("vs", False), 15: ("sv", True)}
GROUPS = ((0, 1, 2, 3), (4, 5, 6, 7), (8, 9, 10, 11), (12, 13), (14,), (15,))
BANKS = ((0, 4, 1), (4, 8, 1), (8, 16, 2), (9, 13, 2), (13, 16, 2))
V_BANKS = (4,)
Y_SHARES = (15, 0)
PIECES = (384, 384, 256)


def tile_routed_moe_kernel(tc, xT, w, gate, offs, pos1, pos2, out):
    nc = tc.nc
    with ExitStack() as ctx:
        lists = ctx.enter_context(tc.tile_pool(name="lists", bufs=1))
        keep = ctx.enter_context(tc.tile_pool(name="keep", bufs=1))
        psum = ctx.enter_context(tc.psum_pool(name="psum", bufs=1))

        offs_t = lists.tile([P, E * C // 16], U16, name="offs_t")
        xv = xT.rearrange("(a p j) t -> a p j t", p=P, j=PACK)
        xr = {}
        for a in range(PASSES):
            if a in X_WHOLE:
                whole = keep.tile([P, PACK, T], F32, name="xr%d" % a)
                nc.sync.dma_start(out=whole[:], in_=xv[a])
                for h in range(T // HALF):
                    xr[a, h] = whole[:, :, h * HALF:(h + 1) * HALF]
            else:
                for h in range(T // HALF):
                    part = keep.tile([P, PACK, HALF], F32, name="xr%d%d" % (a, h))
                    nc.sync.dma_start(out=part[:], in_=xv[a, :, :, h * HALF:(h + 1) * HALF])
                    xr[a, h] = part[:]
            if a == 0:
                nc.sync.dma_start(offs_t[:], offs)
        wv = w.rearrange("e (a p j) n -> e p a (j n)", p=P, j=PACK)
        wr = {}
        for e in range(E):
            if e in SPLIT:
                for a in range(PASSES):
                    tag = "shared" if (e, a) == Y_SHARES else "wr%d_%d" % (e, a)
                    wr[e, a] = keep.tile([P, PACK * N], F32, name="wr%d_%d" % (e, a), tag=tag, align_bytes=64)
                    nc.sync.dma_start(out=wr[e, a][:], in_=wv[e, :, a, :])
            else:
                wr[e] = keep.tile([P, PASSES, PACK * N], F32, name="wr%d" % e)
                nc.sync.dma_start(out=wr[e][:], in_=wv[e])
        pos1_t = lists.tile([P, T // 16], U16, name="pos1_t")
        nc.sync.dma_start(pos1_t[:], pos1)
        pos2_t = lists.tile([P, T // 16], U16, name="pos2_t")
        nc.sync.dma_start(pos2_t[:], pos2)
        g_t = []
        for r in range(2):
            g_r = keep.tile([P, T], F32, name="g%d" % r)
            nc.sync.dma_start(out=g_r[:], in_=gate[r])
            g_t.append(g_r)

        warm = keep.tile([P, 8], F32, name="warm")
        nc.vector.memset(warm[:], 0.0)
        warm2 = keep.tile([P, 8], F32, name="warm2")
        nc.scalar.copy(out=warm2[:], in_=warm[:])
        xw = [keep.tile([P, T], U32, name="xw%d" % a, align_bytes=64) for a in range(PASSES)]
        xs = keep.tile([P, T], U8, name="xs", align_bytes=64)
        nc.gpsimd.memset(xs[:], 0)

        gw, gs, o_c, where = [], [], [], {}
        s0 = 0
        for c, n_s in enumerate(CHUNKS):
            gw.append([keep.tile([P, n_s], U32, name="gw%d_%d" % (a, c), align_bytes=64) for a in range(PASSES)])
            gs.append(keep.tile([P, n_s], U8, name="gs%d" % c, align_bytes=64))
            o_c.append(offs_t[:, s0 // 16:(s0 + n_s) // 16])
            for e in range(s0 // C, (s0 + n_s) // C):
                where[e] = (c, e * C - s0)
            s0 += n_s

        def tokens(a):
            for h in range(T // HALF):
                xg = keep.tile([P, HALF, PACK], BF16, name="xg%d%d" % (a, h), align_bytes=64)
                n_v = X_VEC[a][h]
                if n_v > 0:
                    nc.vector.tensor_copy(
                        out=xg[:, 0:n_v, :].rearrange("p (c i) j -> p c j i", i=4),
                        in_=xr[a, h][:, :, 0:n_v].rearrange("p j (c i) -> p c j i", i=4),
                    )
                nc.scalar.copy(
                    out=xg[:, n_v:HALF, :].rearrange("p (c i) j -> p c j i", i=4),
                    in_=xr[a, h][:, :, n_v:HALF].rearrange("p j (c i) -> p c j i", i=4),
                )
                cols = slice(h * HALF, (h + 1) * HALF)
                nc.vector.quantize_mx(
                    out=xw[a][:, cols].bitcast(FP8X4),
                    scales=xs[4 * a:P, cols],
                    in_=xg[:].rearrange("p t j -> p (t j)"),
                )

        tokens(0)
        for c in range(len(CHUNKS)):
            nc.vector.tensor_copy(out=gw[c][0][:], in_=xw[0][:].indirect(o_c[c]))
        tokens(1)
        for c in range(len(CHUNKS)):
            nc.vector.tensor_copy(out=gw[c][1][:], in_=xw[1][:].indirect(o_c[c]))
            nc.vector.tensor_copy(out=gs[c][:], in_=xs[:].indirect(o_c[c]))

        acc, place = [], {}
        for b, (first, end, step) in enumerate(BANKS):
            experts = list(range(first, end, step))
            acc.append(psum.tile([P, len(experts), C], F32, name="acc%d" % b))
            for i, e in enumerate(experts):
                place[e] = (b, i)
        for gi, grp in enumerate(GROUPS):
            n_e = len(grp)
            wg = keep.tile([P, n_e, PASSES, N * PACK], BF16, name="wg%d" % gi, align_bytes=64)
            wc = keep.tile([P, n_e, PASSES, N], U32, name="wc%d" % gi, align_bytes=64)
            ws = keep.tile([P, n_e, PASSES, N], U8, name="ws%d" % gi, align_bytes=64)
            for i, e in enumerate(grp):
                if e in SPLIT:
                    for a in range(PASSES):
                        dst = wg[:, i, a, :].rearrange("p (c i j) -> p c j i", i=4, j=PACK)
                        src = wr[e, a][:].rearrange("p (j c i) -> p c j i", i=4, j=PACK)
                        if SPLIT[e][0][a] == "v":
                            nc.vector.tensor_copy(out=dst, in_=src)
                        else:
                            nc.scalar.copy(out=dst, in_=src)
                        if SPLIT[e][1]:
                            nc.vector.quantize_mx(
                                out=wc[:, i, a, :].bitcast(FP8X4), scales=ws[:, i, a, :], in_=wg[:, i, a, :]
                            )
                elif e in G_EXPERTS:
                    nc.gpsimd.tensor_scalar(
                        out=wg[:, i, :, :].rearrange("p a (n j) -> p a n j", j=PACK),
                        in0=wr[e][:].rearrange("p a (j n) -> p a n j", j=PACK),
                        scalar1=1.0, scalar2=0.0, op0=MULT, op1=ADD,
                    )
                else:
                    dst = wg[:, i, :, :].rearrange("p a (c i j) -> p a c j i", i=4, j=PACK)
                    src = wr[e][:].rearrange("p a (j c i) -> p a c j i", i=4, j=PACK)
                    if e in V_EXPERTS:
                        nc.vector.tensor_copy(out=dst, in_=src)
                    else:
                        nc.scalar.copy(out=dst, in_=src)
            if grp[0] not in SPLIT or not SPLIT[grp[0]][1]:
                nc.vector.quantize_mx(
                    out=wc[:].rearrange("p e a n -> p (e a n)").bitcast(FP8X4),
                    scales=ws[:].rearrange("p e a n -> p (e a n)"),
                    in_=wg[:].rearrange("p e a m -> p (e a m)"),
                )
            for i, e in enumerate(grp):
                c, s = where[e]
                b, slot = place[e]
                for a in range(PASSES):
                    nc.tensor.matmul_mx(
                        out=acc[b][:, slot, :],
                        lhsT=wc[:, i, a, :].bitcast(FP8X4),
                        lhsT_scale=ws[:, i, a, :],
                        rhs=gw[c][a][:, s:s + C].bitcast(FP8X4),
                        rhs_scale=gs[c][4 * a:P, s:s + C],
                        start=(a == 0),
                        stop=(a == PASSES - 1),
                    )

        y = keep.tile([P, E * C], F32, name="y", tag="shared", align_bytes=64)
        y_by_expert = y[:].rearrange("p (e c) -> p e c", c=C)
        for b, (first, end, step) in enumerate(BANKS):
            if b in V_BANKS:
                nc.vector.tensor_copy(out=y_by_expert[:, first:end:step], in_=acc[b][:])
            else:
                nc.scalar.copy(out=y_by_expert[:, first:end:step], in_=acc[b][:])

        t1 = keep.tile([P, T], F32, name="t1")
        t2 = keep.tile([P, T], F32, name="t2")
        res = keep.tile([P, T], F32, name="res")
        nc.vector.tensor_tensor(out=t1[:], in0=y[:].indirect(pos1_t[:]), in1=g_t[0][:], op=MULT)
        nc.vector.tensor_tensor(out=t2[:], in0=y[:].indirect(pos2_t[:]), in1=g_t[1][:], op=MULT)
        t0 = 0
        for n_t in PIECES:
            cols = slice(t0, t0 + n_t)
            nc.vector.tensor_tensor(out=res[:, cols], in0=t1[:, cols], in1=t2[:, cols], op=ADD)
            nc.sync.dma_start(out=out[:, cols], in_=res[:, cols])
            t0 += n_t
